import numpy as np, ml_dtypes
CORES = [24,27,29,56,59,61,88,91,93,120,123,125]
N = 12
G1 = [0,1,2,3,4,5,6,7,8,9,10,11]
G2 = [0,3,6,9]
G3 = [1,3,5,7,9,11]
def setup_inputs(rng):
    return {"x1": rng.standard_normal((N, 128, 1020), dtype=np.float32).astype(ml_dtypes.bfloat16), "x2": rng.standard_normal((N, 128, 2), dtype=np.float32), "x3": rng.standard_normal((N, 128, 32), dtype=np.float32)}
def reference(x1, x2, x3):
    out = {}
    y = np.full((N, 128, 85), np.nan, x1.dtype)
    s = x1[G1].sum(axis=0, dtype=np.float64).astype(x1.dtype)
    for i, r in enumerate(G1):
        y[r] = s[:, 85 * i:85 * i + 85]
    out["y1"] = y
    y = np.full((N, 128, 8), np.nan, x2.dtype)
    s = np.concatenate([x2[r] for r in G2], axis=1)
    for r in G2:
        y[r] = s
    out["y2"] = y
    y = np.full((N, 128, 32), np.nan, x3.dtype)
    s = x3[G3].max(axis=0)
    for r in G3:
        y[r] = s
    out["y3"] = y
    return out

@@ -1,0 +1,178 @@
+from concourse.bass import DstId, RemoteDMATransfer
+
+SCRATCH = {
+    "xd": ("dram", [4, 128, 255], "bfloat16"),
+    "fl": ("dram", [3, 128, 255], "bfloat16"),
+    "gl": ("dram", [4, 128, 255], "bfloat16"),
+    "yl": ("dram", [128, 255], "bfloat16"),
+    "x2g": ("sbuf", [128, 8], "float32"),
+    "x3d": ("dram", [128, 32], "float32"),
+    "h3": ("dram", [6, 128, 32], "float32"),
+    "y3l": ("dram", [128, 32], "float32"),
+}
+SEMAPHORES = ["x1", "x2", "x3", "sent", "f_in", "g_in", "y1_in", "y2_in", "h_in", "y3_in", "stored"]
+
+ADD, MAX = 1, 2
+
+
+def _engines(mask):
+    return [1 << b for b in range(mask.bit_length()) if (mask >> b) & 1]
+
+
+def _count(mask):
+    return len(_engines(mask))
+
+
+def _split(mask, parts):
+    es = _engines(mask)
+    size = 1
+    while size * 2 * parts <= len(es):
+        size *= 2
+    return [sum(es[i * size:(i + 1) * size]) for i in range(parts)]
+
+
+def _common(topo, src, dsts):
+    m = topo.mask(src, dsts[0])
+    for c in dsts:
+        m &= topo.mask(src, c)
+    return m
+
+
+def _plan(T, topo):
+    m1 = [T.cores[r] for r in T.tables["G1"]]
+    chips = []
+    for c in m1:
+        if topo.chip(c) not in chips:
+            chips.append(topo.chip(c))
+    on = [[c for c in m1 if topo.chip(c) == ch] for ch in chips]
+    fold, gather = [], []
+    for ch in chips:
+        free = [c for c in range(topo.CHIPS * topo.CORES_PER_CHIP) if topo.chip(c) == ch and c not in T.cores]
+        dies = sorted({topo.die(c) for c in free}, key=lambda d: -len([c for c in free if topo.die(c) == d]))
+        a = [c for c in free if topo.die(c) == dies[0]]
+        b = [c for c in free if topo.die(c) == dies[1]]
+        fold.append({1: a[0], 2: a[1], 3: b[0], 0: b[1]})
+        gather.append(a[2])
+    m3 = [T.cores[r] for r in T.tables["G3"]]
+    best = max(range(len(chips)), key=lambda i: len([c for c in m3 if topo.chip(c) == chips[i]]))
+    return m1, chips, on, fold, gather, m3, fold[best][0]
+
+
+def _dst(topo, c):
+    rid, pid, _ = topo.addr(c)
+    return DstId(rid=rid, pnc=pid)
+
+
+def rank_program(g, core, T, topo):
+    m1, chips, on, fold, gather, m3, hmax = _plan(T, topo)
+    m2 = [T.cores[r] for r in T.tables["G2"]]
+    nch = len(chips)
+    if topo.chip(core) not in chips:
+        return
+    ci = chips.index(topo.chip(core))
+    sem = T.sem
+    sent = 0
+    stored = 0
+    w = T.y1.shape[1]
+
+    def hop1_masks(src):
+        return _split(_common(topo, src, [fold[ci][o] for o in range(nch)]), nch)
+
+    if core in T.cores:
+        k = on[ci].index(core)
+        for n, o in enumerate([1, 2, 3, 0]):
+            b = (ci + o) % nch
+            c0 = w * m1.index(on[b][0])
+            q = g.sync if n % 2 == 0 else g.scalar
+            q.dma_start(T.xd[b], T.x1[:, c0:c0 + w * len(on[b])]).then_inc(sem.x1, 16)
+        if core in m3:
+            g.sync.dma_start(T.x3d[:], T.x3[:]).then_inc(sem.x3, 16)
+        if core in m2:
+            i2 = m2.index(core)
+            g.scalar.dma_start(T.x2g[:, 2 * i2:2 * i2 + 2], T.x2[:]).then_inc(sem.x2, 16)
+
+        g.wait_ge(sem.x1, 16 * nch)
+        masks = hop1_masks(core)
+        g.remote_dma_fused(
+            [RemoteDMATransfer(dst_ids=[_dst(topo, fold[ci][o])], dma_engine_mask=masks[o], remote_sem=sem.f_in,
+                               src=T.xd[(ci + o) % nch], dst=T.fl[k]) for o in range(nch)],
+            local_sem=sem.sent)
+        sent += sum(_count(m) for m in masks)
+
+        if core in m3:
+            g.wait_ge(sem.x3, 16)
+            rid, pid, _ = topo.addr(hmax)
+            m = topo.mask(core, hmax)
+            g.remote_dma(T.h3[m3.index(core)], T.x3d[:], sem.h_in, sem.sent, pid, rid, m)
+            sent += _count(m)
+
+        if core in m2:
+            g.wait_ge(sem.x2, 16)
+            others = [c for c in m2 if c != core]
+            m = _common(topo, core, others)
+            sl = T.x2g[:, 2 * i2:2 * i2 + 2]
+            g.remote_dma_fused(
+                [RemoteDMATransfer(dst_ids=[_dst(topo, c) for c in others], dma_engine_mask=m, remote_sem=sem.y2_in,
+                                   srcs=[sl], dsts=[sl for c in others])],
+                local_sem=sem.sent)
+            sent += _count(m)
+            need = sum(_count(_common(topo, c, [c2 for c2 in m2 if c2 != c])) for c in others)
+            g.scalar.wait_ge(sem.x2, 16)
+            g.scalar.wait_ge(sem.y2_in, need)
+            g.scalar.dma_start(T.y2[:], T.x2g[:]).then_inc(sem.stored, 16)
+            stored += 16
+
+        if core in m3:
+            off = [c for c in m3 if topo.chip(c) != topo.chip(hmax)]
+            m_off = _common(topo, hmax, off)
+            m_in = m_off if core in off else topo.mask(hmax, core) & ~m_off
+            g.scalar.wait_ge(sem.y3_in, _count(m_in))
+            g.scalar.dma_start(T.y3[:], T.y3l[:]).then_inc(sem.stored, 16)
+            stored += 16
+
+        g.sync.wait_ge(sem.y1_in, _count(_common(topo, gather[ci], on[ci])))
+        g.sync.dma_start(T.y1[:], T.yl[:, w * k:w * k + w]).then_inc(sem.stored, 16)
+        stored += 16
+
+        g.wait_ge(sem.sent, sent)
+        g.wait_ge(sem.stored, stored)
+        return
+
+    for o in range(nch):
+        if fold[ci][o] == core:
+            g.wait_ge(sem.f_in, sum(_count(hop1_masks(r)[o]) for r in on[ci]))
+            to = gather[(ci + o) % nch]
+            m = topo.mask(core, to)
+            g.remote_dma_fused(
+                [RemoteDMATransfer(dst_ids=[_dst(topo, to)], dma_engine_mask=m, remote_sem=sem.g_in,
+                                   srcs=[T.fl[k] for k in range(len(on[ci]))], dsts=[T.gl[ci]], alu_op=ADD)],
+                local_sem=sem.sent)
+            sent += _count(m)
+
+    if core == hmax:
+        g.wait_ge(sem.h_in, sum(_count(topo.mask(c, core)) for c in m3))
+        off = [c for c in m3 if topo.chip(c) != topo.chip(core)]
+        near = [c for c in m3 if topo.chip(c) == topo.chip(core)]
+        m_off = _common(topo, core, off)
+        srcs = [T.h3[i] for i in range(len(m3))]
+        tr = [RemoteDMATransfer(dst_ids=[_dst(topo, c) for c in off], dma_engine_mask=m_off, remote_sem=sem.y3_in,
+                                srcs=srcs, dsts=[T.y3l[:] for c in off], alu_op=MAX)]
+        sent += _count(m_off)
+        if near:
+            m_on = _common(topo, core, near) & ~m_off
+            tr.append(RemoteDMATransfer(dst_ids=[_dst(topo, c) for c in near], dma_engine_mask=m_on,
+                                        remote_sem=sem.y3_in, srcs=srcs, dsts=[T.y3l[:] for c in near], alu_op=MAX))
+            sent += _count(m_on)
+        g.remote_dma_fused(tr, local_sem=sem.sent)
+
+    if core == gather[ci]:
+        g.wait_ge(sem.g_in, sum(_count(topo.mask(fold[s][(ci - s) % nch], core)) for s in range(nch)))
+        m = _common(topo, core, on[ci])
+        g.remote_dma_fused(
+            [RemoteDMATransfer(dst_ids=[_dst(topo, c) for c in on[ci]], dma_engine_mask=m, remote_sem=sem.y1_in,
+                               srcs=[T.gl[s] for s in range(nch)], dsts=[T.yl[:] for c in on[ci]], alu_op=ADD)],
+            local_sem=sem.sent)
+        sent += _count(m)
+
+    if sent:
+        g.wait_ge(sem.sent, sent)

@@ -1,18 +1,20 @@
 from concourse.bass import DstId, RemoteDMATransfer
 
+NH = 4
 SCRATCH = {
-    "xd": ("dram", [4, 128, 255], "bfloat16"),
-    "fl": ("dram", [3, 128, 255], "bfloat16"),
-    "gl": ("dram", [4, 128, 255], "bfloat16"),
-    "yl": ("dram", [128, 255], "bfloat16"),
-    "x2g": ("sbuf", [128, 8], "float32"),
-    "x3d": ("dram", [128, 32], "float32"),
-    "h3": ("dram", [6, 128, 32], "float32"),
-    "y3l": ("dram", [128, 32], "float32"),
+    "xd": ("dram", [4, 3, 128, 85], "bfloat16"),
+    "fl": ("dram", [6, 128, 85], "bfloat16"),
+    "gl": ("dram", [6, 128, 85], "bfloat16"),
+    "yl": ("dram", [384, 85], "bfloat16"),
+    "l2": ("dram", [4, 128, 2], "float32"),
+    "x3d": ("dram", [NH, 128, 32 // NH], "float32"),
+    "h3": ("dram", [6, 128, 32 // NH], "float32"),
+    "y3l": ("dram", [NH, 128, 32 // NH], "float32"),
 }
 SEMAPHORES = ["x1", "x2", "x3", "sent", "f_in", "g_in", "y1_in", "y2_in", "h_in", "y3_in", "stored"]
 
 ADD, MAX = 1, 2
+NT = 3
 
 
 def _engines(mask):
@@ -40,22 +42,25 @@ def _common(topo, src, dsts):
 
 def _plan(T, topo):
     m1 = [T.cores[r] for r in T.tables["G1"]]
+    every = range(topo.CHIPS * topo.CORES_PER_CHIP)
     chips = []
     for c in m1:
         if topo.chip(c) not in chips:
             chips.append(topo.chip(c))
     on = [[c for c in m1 if topo.chip(c) == ch] for ch in chips]
-    fold, gather = [], []
+    free = []
     for ch in chips:
-        free = [c for c in range(topo.CHIPS * topo.CORES_PER_CHIP) if topo.chip(c) == ch and c not in T.cores]
-        dies = sorted({topo.die(c) for c in free}, key=lambda d: -len([c for c in free if topo.die(c) == d]))
-        a = [c for c in free if topo.die(c) == dies[0]]
-        b = [c for c in free if topo.die(c) == dies[1]]
-        fold.append({1: a[0], 2: a[1], 3: b[0], 0: b[1]})
-        gather.append(a[2])
-    m3 = [T.cores[r] for r in T.tables["G3"]]
-    best = max(range(len(chips)), key=lambda i: len([c for c in m3 if topo.chip(c) == chips[i]]))
-    return m1, chips, on, fold, gather, m3, fold[best][0]
+        f = [c for c in every if topo.chip(c) == ch and c not in T.cores]
+        dies = sorted({topo.die(c) for c in f}, key=lambda d: len([c for c in f if topo.die(c) == d]))
+        b = [c for c in f if topo.die(c) == dies[0]]
+        a = [c for c in f if topo.die(c) == dies[1]]
+        free.append([b[0], a[0], b[1], a[1], a[2]])
+    hs = []
+    for c in every:
+        if topo.chip(c) not in chips and topo.same_plane(topo.chip(c), chips[0]):
+            if not [x for x in hs if topo.chip(x) == topo.chip(c) and topo.die(x) == topo.die(c)]:
+                hs.append(c)
+    return m1, chips, on, free, hs[:NH]
 
 
 def _dst(topo, c):
@@ -64,19 +69,46 @@ def _dst(topo, c):
 
 
 def rank_program(g, core, T, topo):
-    m1, chips, on, fold, gather, m3, hmax = _plan(T, topo)
+    m1, chips, on, free, hs = _plan(T, topo)
     m2 = [T.cores[r] for r in T.tables["G2"]]
+    m3 = [T.cores[r] for r in T.tables["G3"]]
     nch = len(chips)
-    if topo.chip(core) not in chips:
-        return
-    ci = chips.index(topo.chip(core))
     sem = T.sem
     sent = 0
     stored = 0
-    w = T.y1.shape[1]
+    far = [(o, t) for o in range(1, nch) for t in range(NT)]
+    pairs = len(far) // 2
 
-    def hop1_masks(src):
-        return _split(_common(topo, src, [fold[ci][o] for o in range(nch)]), nch)
+    def rank_engines(r):
+        m_on = _common(topo, r, free[chips.index(topo.chip(r))])
+        m_out = _common(topo, r, hs)
+        es = _engines(m_on & ~m_out) + _engines(m_on & m_out)[::-1]
+        n = len(far) + NT
+        return es[:n], sum(es[n:])
+
+    if core in hs:
+        q = hs.index(core)
+        g.wait_ge(sem.h_in, sum(_count(_split(rank_engines(c)[1], NH)[q]) for c in m3))
+        m = _common(topo, core, m3)
+        g.remote_dma_fused(
+            [RemoteDMATransfer(dst_ids=[_dst(topo, c) for c in m3], dma_engine_mask=m, remote_sem=sem.y3_in,
+                               srcs=[T.h3[i] for i in range(len(m3))], dsts=[T.y3l[q] for c in m3], alu_op=MAX)],
+            local_sem=sem.sent)
+        g.wait_ge(sem.sent, _count(m))
+        return
+    if topo.chip(core) not in chips:
+        return
+
+    ci = chips.index(topo.chip(core))
+    w = T.y1.shape[1]
+    nr = len(on[ci])
+    here = free[ci]
+
+    def hop2_mask(s, i):
+        o, t = far[i]
+        src = free[s][min(i // 2, pairs)]
+        m = topo.mask(src, free[(s + o) % nch][t])
+        return _split(m, 2)[i % 2] if i // 2 < pairs else m
 
     if core in T.cores:
         k = on[ci].index(core)
@@ -89,90 +121,76 @@ def rank_program(g, core, T, topo):
             g.sync.dma_start(T.x3d[:], T.x3[:]).then_inc(sem.x3, 16)
         if core in m2:
             i2 = m2.index(core)
-            g.scalar.dma_start(T.x2g[:, 2 * i2:2 * i2 + 2], T.x2[:]).then_inc(sem.x2, 16)
+            g.scalar.dma_start(T.l2[i2], T.x2[:]).then_inc(sem.x2, 16)
 
         g.wait_ge(sem.x1, 16 * nch)
-        masks = hop1_masks(core)
+        ms, m_small = rank_engines(core)
         g.remote_dma_fused(
-            [RemoteDMATransfer(dst_ids=[_dst(topo, fold[ci][o])], dma_engine_mask=masks[o], remote_sem=sem.f_in,
-                               src=T.xd[(ci + o) % nch], dst=T.fl[k]) for o in range(nch)],
+            [RemoteDMATransfer(dst_ids=[_dst(topo, here[min(i // 2, pairs)])], dma_engine_mask=ms[i],
+                               remote_sem=sem.f_in, src=T.xd[(ci + far[i][0]) % nch, far[i][1]],
+                               dst=T.fl[2 * k + i % 2]) for i in range(len(far))] +
+            [RemoteDMATransfer(dst_ids=[_dst(topo, here[t])], dma_engine_mask=ms[len(far) + t], remote_sem=sem.g_in,
+                               src=T.xd[ci, t], dst=T.gl[nch - 1 + k]) for t in range(NT)],
             local_sem=sem.sent)
-        sent += sum(_count(m) for m in masks)
+        sent += len(ms)
 
         if core in m3:
             g.wait_ge(sem.x3, 16)
-            rid, pid, _ = topo.addr(hmax)
-            m = topo.mask(core, hmax)
-            g.remote_dma(T.h3[m3.index(core)], T.x3d[:], sem.h_in, sem.sent, pid, rid, m)
-            sent += _count(m)
+            parts = _split(m_small, NH)
+            g.remote_dma_fused(
+                [RemoteDMATransfer(dst_ids=[_dst(topo, hs[q])], dma_engine_mask=parts[q], remote_sem=sem.h_in,
+                                   src=T.x3d[q], dst=T.h3[m3.index(core)]) for q in range(NH)],
+                local_sem=sem.sent)
+            sent += sum(_count(m) for m in parts)
 
         if core in m2:
             g.wait_ge(sem.x2, 16)
             others = [c for c in m2 if c != core]
-            m = _common(topo, core, others)
-            sl = T.x2g[:, 2 * i2:2 * i2 + 2]
             g.remote_dma_fused(
-                [RemoteDMATransfer(dst_ids=[_dst(topo, c) for c in others], dma_engine_mask=m, remote_sem=sem.y2_in,
-                                   srcs=[sl], dsts=[sl for c in others])],
+                [RemoteDMATransfer(dst_ids=[_dst(topo, c) for c in others], dma_engine_mask=m_small,
+                                   remote_sem=sem.y2_in, srcs=[T.l2[i2]], dsts=[T.l2[i2] for c in others])],
                 local_sem=sem.sent)
-            sent += _count(m)
-            need = sum(_count(_common(topo, c, [c2 for c2 in m2 if c2 != c])) for c in others)
+            sent += _count(m_small)
             g.scalar.wait_ge(sem.x2, 16)
-            g.scalar.wait_ge(sem.y2_in, need)
-            g.scalar.dma_start(T.y2[:], T.x2g[:]).then_inc(sem.stored, 16)
-            stored += 16
+            g.scalar.wait_ge(sem.y2_in, sum(_count(rank_engines(c)[1]) for c in others))
+            for j in range(len(m2)):
+                g.scalar.dma_start(T.y2[:, 2 * j:2 * j + 2], T.l2[j]).then_inc(sem.stored, 16)
+                stored += 16
 
         if core in m3:
-            off = [c for c in m3 if topo.chip(c) != topo.chip(hmax)]
-            m_off = _common(topo, hmax, off)
-            m_in = m_off if core in off else topo.mask(hmax, core) & ~m_off
-            g.scalar.wait_ge(sem.y3_in, _count(m_in))
+            g.scalar.wait_ge(sem.y3_in, sum(_count(_common(topo, x, m3)) for x in hs))
             g.scalar.dma_start(T.y3[:], T.y3l[:]).then_inc(sem.stored, 16)
             stored += 16
 
-        g.sync.wait_ge(sem.y1_in, _count(_common(topo, gather[ci], on[ci])))
-        g.sync.dma_start(T.y1[:], T.yl[:, w * k:w * k + w]).then_inc(sem.stored, 16)
+        g.sync.wait_ge(sem.y1_in, sum(_count(_common(topo, c, on[ci])) for c in here[:NT]))
+        g.sync.dma_start(T.y1[:], T.yl[k::nr, :]).then_inc(sem.stored, 16)
         stored += 16
 
         g.wait_ge(sem.sent, sent)
         g.wait_ge(sem.stored, stored)
         return
 
-    for o in range(nch):
-        if fold[ci][o] == core:
-            g.wait_ge(sem.f_in, sum(_count(hop1_masks(r)[o]) for r in on[ci]))
-            to = gather[(ci + o) % nch]
-            m = topo.mask(core, to)
-            g.remote_dma_fused(
-                [RemoteDMATransfer(dst_ids=[_dst(topo, to)], dma_engine_mask=m, remote_sem=sem.g_in,
-                                   srcs=[T.fl[k] for k in range(len(on[ci]))], dsts=[T.gl[ci]], alu_op=ADD)],
-                local_sem=sem.sent)
-            sent += _count(m)
+    h = here.index(core)
 
-    if core == hmax:
-        g.wait_ge(sem.h_in, sum(_count(topo.mask(c, core)) for c in m3))
-        off = [c for c in m3 if topo.chip(c) != topo.chip(core)]
-        near = [c for c in m3 if topo.chip(c) == topo.chip(core)]
-        m_off = _common(topo, core, off)
-        srcs = [T.h3[i] for i in range(len(m3))]
-        tr = [RemoteDMATransfer(dst_ids=[_dst(topo, c) for c in off], dma_engine_mask=m_off, remote_sem=sem.y3_in,
-                                srcs=srcs, dsts=[T.y3l[:] for c in off], alu_op=MAX)]
-        sent += _count(m_off)
-        if near:
-            m_on = _common(topo, core, near) & ~m_off
-            tr.append(RemoteDMATransfer(dst_ids=[_dst(topo, c) for c in near], dma_engine_mask=m_on,
-                                        remote_sem=sem.y3_in, srcs=srcs, dsts=[T.y3l[:] for c in near], alu_op=MAX))
-            sent += _count(m_on)
-        g.remote_dma_fused(tr, local_sem=sem.sent)
+    mine = [i for i in range(len(far)) if min(i // 2, pairs) == h]
+    g.wait_ge(sem.f_in, nr * len(mine))
+    g.remote_dma_fused(
+        [RemoteDMATransfer(dst_ids=[_dst(topo, free[(ci + far[i][0]) % nch][far[i][1]])],
+                           dma_engine_mask=hop2_mask(ci, i), remote_sem=sem.g_in,
+                           srcs=[T.fl[2 * r + i % 2] for r in range(nr)], dsts=[T.gl[far[i][0] - 1]], alu_op=ADD)
+         for i in mine],
+        local_sem=sem.sent)
+    sent += sum(_count(hop2_mask(ci, i)) for i in mine)
 
-    if core == gather[ci]:
-        g.wait_ge(sem.g_in, sum(_count(topo.mask(fold[s][(ci - s) % nch], core)) for s in range(nch)))
+    if h < NT:
+        need = nr + sum(_count(hop2_mask((ci - o) % nch, i)) for i, (o, t) in enumerate(far) if t == h)
+        g.wait_ge(sem.g_in, need)
         m = _common(topo, core, on[ci])
         g.remote_dma_fused(
             [RemoteDMATransfer(dst_ids=[_dst(topo, c) for c in on[ci]], dma_engine_mask=m, remote_sem=sem.y1_in,
-                               srcs=[T.gl[s] for s in range(nch)], dsts=[T.yl[:] for c in on[ci]], alu_op=ADD)],
+                               srcs=[T.gl[i] for i in range(nch - 1 + nr)],
+                               dsts=[T.yl[128 * h:128 * h + 128, :] for c in on[ci]], alu_op=ADD)],
             local_sem=sem.sent)
         sent += _count(m)
 
-    if sent:
-        g.wait_ge(sem.sent, sent)
+    g.wait_ge(sem.sent, sent)

@@ -11,7 +11,7 @@ SCRATCH = {
     "h3": ("dram", [6, 128, 32 // NH], "float32"),
     "y3l": ("dram", [NH, 128, 32 // NH], "float32"),
 }
-SEMAPHORES = ["x1", "x2", "x3", "sent", "f_in", "g_in", "y1_in", "y2_in", "h_in", "y3_in", "stored"]
+SEMAPHORES = ["x1a", "x1b", "x2", "x3", "sent", "f_in", "g_in", "y1_in", "y2_in", "h_in", "y3_in", "stored"]
 
 ADD, MAX = 1, 2
 NT = 3
@@ -78,13 +78,14 @@ def rank_program(g, core, T, topo):
     stored = 0
     far = [(o, t) for o in range(1, nch) for t in range(NT)]
     pairs = len(far) // 2
+    early = 2 * NT
 
     def rank_engines(r):
         m_on = _common(topo, r, free[chips.index(topo.chip(r))])
         m_out = _common(topo, r, hs)
         es = _engines(m_on & ~m_out) + _engines(m_on & m_out)[::-1]
-        n = len(far) + NT
-        return es[:n], sum(es[n:])
+        n = len(es) - NH
+        return _split(sum(es[:n]), early), sum(es[n:])
 
     if core in hs:
         q = hs.index(core)
@@ -104,6 +105,9 @@ def rank_program(g, core, T, topo):
     nr = len(on[ci])
     here = free[ci]
 
+    def hop1_mask(r, i):
+        return rank_engines(r)[0][i % early]
+
     def hop2_mask(s, i):
         o, t = far[i]
         src = free[s][min(i // 2, pairs)]
@@ -116,23 +120,28 @@ def rank_program(g, core, T, topo):
             b = (ci + o) % nch
             c0 = w * m1.index(on[b][0])
             q = g.sync if n % 2 == 0 else g.scalar
-            q.dma_start(T.xd[b], T.x1[:, c0:c0 + w * len(on[b])]).then_inc(sem.x1, 16)
+            q.dma_start(T.xd[b], T.x1[:, c0:c0 + w * len(on[b])]).then_inc(sem.x1a if n < 2 else sem.x1b, 16)
         if core in m3:
             g.sync.dma_start(T.x3d[:], T.x3[:]).then_inc(sem.x3, 16)
         if core in m2:
             i2 = m2.index(core)
             g.scalar.dma_start(T.l2[i2], T.x2[:]).then_inc(sem.x2, 16)
 
-        g.wait_ge(sem.x1, 16 * nch)
-        ms, m_small = rank_engines(core)
+        def to_fold(i):
+            return RemoteDMATransfer(dst_ids=[_dst(topo, here[min(i // 2, pairs)])], dma_engine_mask=hop1_mask(core, i),
+                                     remote_sem=sem.f_in, src=T.xd[(ci + far[i][0]) % nch, far[i][1]],
+                                     dst=T.fl[2 * k + i % 2])
+
+        g.wait_ge(sem.x1a, 32)
+        g.remote_dma_fused([to_fold(i) for i in range(early)], local_sem=sem.sent)
+        g.wait_ge(sem.x1b, 32)
         g.remote_dma_fused(
-            [RemoteDMATransfer(dst_ids=[_dst(topo, here[min(i // 2, pairs)])], dma_engine_mask=ms[i],
-                               remote_sem=sem.f_in, src=T.xd[(ci + far[i][0]) % nch, far[i][1]],
-                               dst=T.fl[2 * k + i % 2]) for i in range(len(far))] +
-            [RemoteDMATransfer(dst_ids=[_dst(topo, here[t])], dma_engine_mask=ms[len(far) + t], remote_sem=sem.g_in,
-                               src=T.xd[ci, t], dst=T.gl[nch - 1 + k]) for t in range(NT)],
+            [to_fold(i) for i in range(early, len(far))] +
+            [RemoteDMATransfer(dst_ids=[_dst(topo, here[t])], dma_engine_mask=hop1_mask(core, len(far) + t),
+                               remote_sem=sem.g_in, src=T.xd[ci, t], dst=T.gl[nch - 1 + k]) for t in range(NT)],
             local_sem=sem.sent)
-        sent += len(ms)
+        sent += sum(_count(hop1_mask(core, i)) for i in range(len(far) + NT))
+        m_small = rank_engines(core)[1]
 
         if core in m3:
             g.wait_ge(sem.x3, 16)
@@ -173,7 +182,7 @@ def rank_program(g, core, T, topo):
     h = here.index(core)
 
     mine = [i for i in range(len(far)) if min(i // 2, pairs) == h]
-    g.wait_ge(sem.f_in, nr * len(mine))
+    g.wait_ge(sem.f_in, sum(_count(hop1_mask(r, i)) for r in on[ci] for i in mine))
     g.remote_dma_fused(
         [RemoteDMATransfer(dst_ids=[_dst(topo, free[(ci + far[i][0]) % nch][far[i][1]])],
                            dma_engine_mask=hop2_mask(ci, i), remote_sem=sem.g_in,
@@ -183,7 +192,8 @@ def rank_program(g, core, T, topo):
     sent += sum(_count(hop2_mask(ci, i)) for i in mine)
 
     if h < NT:
-        need = nr + sum(_count(hop2_mask((ci - o) % nch, i)) for i, (o, t) in enumerate(far) if t == h)
+        need = sum(_count(hop1_mask(r, len(far) + h)) for r in on[ci])
+        need += sum(_count(hop2_mask((ci - o) % nch, i)) for i, (o, t) in enumerate(far) if t == h)
         g.wait_ge(sem.g_in, need)
         m = _common(topo, core, on[ci])
         g.remote_dma_fused(

@@ -11,10 +11,21 @@ SCRATCH = {
     "h3": ("dram", [6, 128, 32 // NH], "float32"),
     "y3l": ("dram", [NH, 128, 32 // NH], "float32"),
 }
-SEMAPHORES = ["x1a", "x1b", "x2", "x3", "sent", "f_in", "g_in", "y1_in", "y2_in", "h_in", "y3_in", "stored"]
+SEMAPHORES = ["x1a", "x1b", "x2", "x3", "sent", "f_in0", "f_in1", "g_in", "y1_in", "y2_in", "h_in", "y3_in", "stored"]
 
 ADD, MAX = 1, 2
 NT = 3
+JOBS = [[[0, 1]], [[2, 3]], [[4], [6]], [[5], [7]], [[8]]]
+
+
+def _where(i):
+    for h, calls in enumerate(JOBS):
+        s = 0
+        for c, call in enumerate(calls):
+            for j in call:
+                if j == i:
+                    return h, c, s
+                s += 1
 
 
 def _engines(mask):
@@ -77,7 +88,6 @@ def rank_program(g, core, T, topo):
     sent = 0
     stored = 0
     far = [(o, t) for o in range(1, nch) for t in range(NT)]
-    pairs = len(far) // 2
     early = 2 * NT
 
     def rank_engines(r):
@@ -104,15 +114,16 @@ def rank_program(g, core, T, topo):
     w = T.y1.shape[1]
     nr = len(on[ci])
     here = free[ci]
+    f_in = [sem.f_in0, sem.f_in1]
 
     def hop1_mask(r, i):
         return rank_engines(r)[0][i % early]
 
     def hop2_mask(s, i):
         o, t = far[i]
-        src = free[s][min(i // 2, pairs)]
-        m = topo.mask(src, free[(s + o) % nch][t])
-        return _split(m, 2)[i % 2] if i // 2 < pairs else m
+        h, c, _ = _where(i)
+        call = JOBS[h][c]
+        return _split(topo.mask(free[s][h], free[(s + o) % nch][t]), len(call))[call.index(i)]
 
     if core in T.cores:
         k = on[ci].index(core)
@@ -128,9 +139,10 @@ def rank_program(g, core, T, topo):
             g.scalar.dma_start(T.l2[i2], T.x2[:]).then_inc(sem.x2, 16)
 
         def to_fold(i):
-            return RemoteDMATransfer(dst_ids=[_dst(topo, here[min(i // 2, pairs)])], dma_engine_mask=hop1_mask(core, i),
-                                     remote_sem=sem.f_in, src=T.xd[(ci + far[i][0]) % nch, far[i][1]],
-                                     dst=T.fl[2 * k + i % 2])
+            h, c, s = _where(i)
+            return RemoteDMATransfer(dst_ids=[_dst(topo, here[h])], dma_engine_mask=hop1_mask(core, i),
+                                     remote_sem=f_in[c], src=T.xd[(ci + far[i][0]) % nch, far[i][1]],
+                                     dst=T.fl[2 * k + s])
 
         g.wait_ge(sem.x1a, 32)
         g.remote_dma_fused([to_fold(i) for i in range(early)], local_sem=sem.sent)
@@ -181,15 +193,16 @@ def rank_program(g, core, T, topo):
 
     h = here.index(core)
 
-    mine = [i for i in range(len(far)) if min(i // 2, pairs) == h]
-    g.wait_ge(sem.f_in, sum(_count(hop1_mask(r, i)) for r in on[ci] for i in mine))
-    g.remote_dma_fused(
-        [RemoteDMATransfer(dst_ids=[_dst(topo, free[(ci + far[i][0]) % nch][far[i][1]])],
-                           dma_engine_mask=hop2_mask(ci, i), remote_sem=sem.g_in,
-                           srcs=[T.fl[2 * r + i % 2] for r in range(nr)], dsts=[T.gl[far[i][0] - 1]], alu_op=ADD)
-         for i in mine],
-        local_sem=sem.sent)
-    sent += sum(_count(hop2_mask(ci, i)) for i in mine)
+    for c, call in enumerate(JOBS[h]):
+        g.wait_ge(f_in[c], sum(_count(hop1_mask(r, i)) for r in on[ci] for i in call))
+        g.remote_dma_fused(
+            [RemoteDMATransfer(dst_ids=[_dst(topo, free[(ci + far[i][0]) % nch][far[i][1]])],
+                               dma_engine_mask=hop2_mask(ci, i), remote_sem=sem.g_in,
+                               srcs=[T.fl[2 * r + _where(i)[2]] for r in range(nr)], dsts=[T.gl[far[i][0] - 1]],
+                               alu_op=ADD)
+             for i in call],
+            local_sem=sem.sent)
+        sent += sum(_count(hop2_mask(ci, i)) for i in call)
 
     if h < NT:
         need = sum(_count(hop1_mask(r, len(far) + h)) for r in on[ci])

from concourse.bass import DstId, RemoteDMATransfer

NH = 4
SCRATCH = {
    "xd": ("dram", [4, 3, 128, 85], "bfloat16"),
    "fl": ("dram", [6, 128, 85], "bfloat16"),
    "gl": ("dram", [6, 128, 85], "bfloat16"),
    "yl": ("dram", [384, 85], "bfloat16"),
    "l2": ("dram", [4, 128, 2], "float32"),
    "x3d": ("dram", [NH, 128, 32 // NH], "float32"),
    "h3": ("dram", [6, 128, 32 // NH], "float32"),
    "y3l": ("dram", [NH, 128, 32 // NH], "float32"),
}
SEMAPHORES = ["x1a", "x1b", "x2", "x3", "sent", "f_in0", "f_in1", "g_in", "y1_in", "y2_in", "h_in", "y3_in", "stored"]

ADD, MAX = 1, 2
NT = 3
JOBS = [[[0, 1]], [[2, 3]], [[4], [6]], [[5], [7]], [[8]]]


def _where(i):
    for h, calls in enumerate(JOBS):
        s = 0
        for c, call in enumerate(calls):
            for j in call:
                if j == i:
                    return h, c, s
                s += 1


def _engines(mask):
    return [1 << b for b in range(mask.bit_length()) if (mask >> b) & 1]


def _count(mask):
    return len(_engines(mask))


def _split(mask, parts):
    es = _engines(mask)
    size = 1
    while size * 2 * parts <= len(es):
        size *= 2
    return [sum(es[i * size:(i + 1) * size]) for i in range(parts)]


def _common(topo, src, dsts):
    m = topo.mask(src, dsts[0])
    for c in dsts:
        m &= topo.mask(src, c)
    return m


def _plan(T, topo):
    m1 = [T.cores[r] for r in T.tables["G1"]]
    every = range(topo.CHIPS * topo.CORES_PER_CHIP)
    chips = []
    for c in m1:
        if topo.chip(c) not in chips:
            chips.append(topo.chip(c))
    on = [[c for c in m1 if topo.chip(c) == ch] for ch in chips]
    free = []
    for ch in chips:
        f = [c for c in every if topo.chip(c) == ch and c not in T.cores]
        dies = sorted({topo.die(c) for c in f}, key=lambda d: len([c for c in f if topo.die(c) == d]))
        b = [c for c in f if topo.die(c) == dies[0]]
        a = [c for c in f if topo.die(c) == dies[1]]
        free.append([b[0], a[0], b[1], a[1], a[2]])
    hs = []
    for c in every:
        if topo.chip(c) not in chips and topo.same_plane(topo.chip(c), chips[0]):
            if not [x for x in hs if topo.chip(x) == topo.chip(c) and topo.die(x) == topo.die(c)]:
                hs.append(c)
    return m1, chips, on, free, hs[:NH]


def _dst(topo, c):
    rid, pid, _ = topo.addr(c)
    return DstId(rid=rid, pnc=pid)


def rank_program(g, core, T, topo):
    m1, chips, on, free, hs = _plan(T, topo)
    m2 = [T.cores[r] for r in T.tables["G2"]]
    m3 = [T.cores[r] for r in T.tables["G3"]]
    nch = len(chips)
    sem = T.sem
    sent = 0
    stored = 0
    far = [(o, t) for o in range(1, nch) for t in range(NT)]
    early = 2 * NT

    def rank_engines(r):
        m_on = _common(topo, r, free[chips.index(topo.chip(r))])
        m_out = _common(topo, r, hs)
        es = _engines(m_on & ~m_out) + _engines(m_on & m_out)[::-1]
        n = len(es) - NH
        return _split(sum(es[:n]), early), sum(es[n:])

    if core in hs:
        q = hs.index(core)
        g.wait_ge(sem.h_in, sum(_count(_split(rank_engines(c)[1], NH)[q]) for c in m3))
        m = _common(topo, core, m3)
        g.remote_dma_fused(
            [RemoteDMATransfer(dst_ids=[_dst(topo, c) for c in m3], dma_engine_mask=m, remote_sem=sem.y3_in,
                               srcs=[T.h3[i] for i in range(len(m3))], dsts=[T.y3l[q] for c in m3], alu_op=MAX)],
            local_sem=sem.sent)
        g.wait_ge(sem.sent, _count(m))
        return
    if topo.chip(core) not in chips:
        return

    ci = chips.index(topo.chip(core))
    w = T.y1.shape[1]
    nr = len(on[ci])
    here = free[ci]
    f_in = [sem.f_in0, sem.f_in1]

    def hop1_mask(r, i):
        return rank_engines(r)[0][i % early]

    def hop2_mask(s, i):
        o, t = far[i]
        h, c, _ = _where(i)
        call = JOBS[h][c]
        return _split(topo.mask(free[s][h], free[(s + o) % nch][t]), len(call))[call.index(i)]

    if core in T.cores:
        k = on[ci].index(core)
        for n, o in enumerate([1, 2, 3, 0]):
            b = (ci + o) % nch
            c0 = w * m1.index(on[b][0])
            q = g.sync if n % 2 == 0 else g.scalar
            q.dma_start(T.xd[b], T.x1[:, c0:c0 + w * len(on[b])]).then_inc(sem.x1a if n < 2 else sem.x1b, 16)
        if core in m3:
            g.sync.dma_start(T.x3d[:], T.x3[:]).then_inc(sem.x3, 16)
        if core in m2:
            i2 = m2.index(core)
            g.scalar.dma_start(T.l2[i2], T.x2[:]).then_inc(sem.x2, 16)

        def to_fold(i):
            h, c, s = _where(i)
            return RemoteDMATransfer(dst_ids=[_dst(topo, here[h])], dma_engine_mask=hop1_mask(core, i),
                                     remote_sem=f_in[c], src=T.xd[(ci + far[i][0]) % nch, far[i][1]],
                                     dst=T.fl[2 * k + s])

        g.wait_ge(sem.x1a, 32)
        g.remote_dma_fused([to_fold(i) for i in range(early)], local_sem=sem.sent)
        g.wait_ge(sem.x1b, 32)
        g.remote_dma_fused(
            [to_fold(i) for i in range(early, len(far))] +
            [RemoteDMATransfer(dst_ids=[_dst(topo, here[t])], dma_engine_mask=hop1_mask(core, len(far) + t),
                               remote_sem=sem.g_in, src=T.xd[ci, t], dst=T.gl[nch - 1 + k]) for t in range(NT)],
            local_sem=sem.sent)
        sent += sum(_count(hop1_mask(core, i)) for i in range(len(far) + NT))
        m_small = rank_engines(core)[1]

        if core in m3:
            g.wait_ge(sem.x3, 16)
            parts = _split(m_small, NH)
            g.remote_dma_fused(
                [RemoteDMATransfer(dst_ids=[_dst(topo, hs[q])], dma_engine_mask=parts[q], remote_sem=sem.h_in,
                                   src=T.x3d[q], dst=T.h3[m3.index(core)]) for q in range(NH)],
                local_sem=sem.sent)
            sent += sum(_count(m) for m in parts)

        if core in m2:
            g.wait_ge(sem.x2, 16)
            others = [c for c in m2 if c != core]
            g.remote_dma_fused(
                [RemoteDMATransfer(dst_ids=[_dst(topo, c) for c in others], dma_engine_mask=m_small,
                                   remote_sem=sem.y2_in, srcs=[T.l2[i2]], dsts=[T.l2[i2] for c in others])],
                local_sem=sem.sent)
            sent += _count(m_small)
            g.scalar.wait_ge(sem.x2, 16)
            g.scalar.wait_ge(sem.y2_in, sum(_count(rank_engines(c)[1]) for c in others))
            for j in range(len(m2)):
                g.scalar.dma_start(T.y2[:, 2 * j:2 * j + 2], T.l2[j]).then_inc(sem.stored, 16)
                stored += 16

        if core in m3:
            g.scalar.wait_ge(sem.y3_in, sum(_count(_common(topo, x, m3)) for x in hs))
            g.scalar.dma_start(T.y3[:], T.y3l[:]).then_inc(sem.stored, 16)
            stored += 16

        g.sync.wait_ge(sem.y1_in, sum(_count(_common(topo, c, on[ci])) for c in here[:NT]))
        g.sync.dma_start(T.y1[:], T.yl[k::nr, :]).then_inc(sem.stored, 16)
        stored += 16

        g.wait_ge(sem.sent, sent)
        g.wait_ge(sem.stored, stored)
        return

    h = here.index(core)

    for c, call in enumerate(JOBS[h]):
        g.wait_ge(f_in[c], sum(_count(hop1_mask(r, i)) for r in on[ci] for i in call))
        g.remote_dma_fused(
            [RemoteDMATransfer(dst_ids=[_dst(topo, free[(ci + far[i][0]) % nch][far[i][1]])],
                               dma_engine_mask=hop2_mask(ci, i), remote_sem=sem.g_in,
                               srcs=[T.fl[2 * r + _where(i)[2]] for r in range(nr)], dsts=[T.gl[far[i][0] - 1]],
                               alu_op=ADD)
             for i in call],
            local_sem=sem.sent)
        sent += sum(_count(hop2_mask(ci, i)) for i in call)

    if h < NT:
        need = sum(_count(hop1_mask(r, len(far) + h)) for r in on[ci])
        need += sum(_count(hop2_mask((ci - o) % nch, i)) for i, (o, t) in enumerate(far) if t == h)
        g.wait_ge(sem.g_in, need)
        m = _common(topo, core, on[ci])
        g.remote_dma_fused(
            [RemoteDMATransfer(dst_ids=[_dst(topo, c) for c in on[ci]], dma_engine_mask=m, remote_sem=sem.y1_in,
                               srcs=[T.gl[i] for i in range(nch - 1 + nr)],
                               dsts=[T.yl[128 * h:128 * h + 128, :] for c in on[ci]], alu_op=ADD)],
            local_sem=sem.sent)
        sent += _count(m)

    g.wait_ge(sem.sent, sent)
